import numpy as np
import ml_dtypes


def mxq(x, axis, fmt="e4m3"):
    dtype, down = {"e4m3": (ml_dtypes.float8_e4m3fn, 7), "e5m2": (ml_dtypes.float8_e5m2, 14)}[fmt]
    v = np.moveaxis(np.asarray(x, np.float32).astype(ml_dtypes.bfloat16).astype(np.float64), axis, -1)
    blocks = v.reshape(v.shape[:-1] + (-1, 32))
    amax = np.abs(blocks).max(-1, keepdims=True)
    byte = np.maximum(np.where(amax > 0, np.frexp(amax)[1] - 1 + 127, 0) - down, 1)
    scale = np.exp2(byte - 127.0)
    codes = (blocks / scale).astype(np.float32).astype(dtype).astype(np.float64)
    return np.moveaxis((codes * scale).reshape(v.shape), -1, axis)


WIDE = False


def mx_kscale(k):
    if not WIDE:
        return np.ones(k)
    levels = np.array([18, -18])
    if k % 512:
        return np.exp2(np.random.permutation(np.resize(levels, k // 32))).repeat(32)
    a = np.empty((k // 512, 16))
    for p in range(k // 512):
        a[p, :8] = np.random.permutation(np.resize(levels, 8))
        for g in range(8):
            far = levels[np.abs(levels - a[p, g]) >= 10]
            a[p, g + 8] = far[np.random.randint(len(far))]
    return np.exp2(a.ravel()).repeat(32)


def f64(x):
    return np.asarray(x).astype(np.float64)


def striped(idx):
    return np.tile(np.asarray(idx).reshape(-1, 16).T, (8, 1)).astype(np.uint16)


def unstriped(offs):
    return offs[:16].T.reshape(-1).astype(np.int64)

def planes(y):
    n, m = y.shape
    v = y.astype(np.float32).astype(ml_dtypes.bfloat16).astype(np.float64).reshape(n // 32, 32, m)
    top = np.abs(v).max(1)
    byte = np.clip(np.where(top > 0, np.frexp(top)[1] - 1 + 127 - 7, 1), 1, 254)
    codes = (v * np.exp2(127.0 - byte)[:, None, :]).reshape(n, m).astype(np.float32).astype(ml_dtypes.float8_e4m3fn).view(np.uint8)
    words = codes.reshape(n // 512, 128, 4, m).transpose(0, 1, 3, 2)
    return np.ascontiguousarray(words), np.ascontiguousarray(byte.astype(np.uint8).reshape(n // 512, 16, m))


V, K, E, D, DV = 512, 2, 1024, 512, 512


def setup_inputs():
    n = np.random.standard_normal
    v = mx_kscale(DV)[:, None]
    coarse = lambda x: x.astype(np.float32).astype(ml_dtypes.bfloat16).astype(np.float64)
    return {
        "dyT": (coarse(n((DV, V))) * v).astype(np.float32),
        "hE": (np.random.randint(1, 32, (DV, E)) / 32.0).astype(np.float32),
        "ew": np.tile(np.random.randint(8, 33, E) / 16.0, (128, 1)).astype(np.float32),
        "wm": (n((DV, D)) / np.sqrt(DV) / v).astype(np.float32),
        "offs": striped(np.random.randint(0, V, E)),
        "offs2": striped(np.random.permutation(E)),
    }


def reference(dyT, hE, ew, wm, offs, offs2):
    h = f64(hE)
    dz = f64(ew)[:1] * f64(dyT)[:, unstriped(offs)] * h * (1.0 - h)
    dm = mxq(f64(wm), 0, "e4m3").T @ mxq(dz, 0, "e5m2")
    out_0 = dm[:, unstriped(offs2)].reshape(D, V, K).sum(-1)
    return (out_0,) + planes(out_0)

@@ -1,0 +1,180 @@
+from contextlib import ExitStack
+
+import concourse.mybir as mybir
+
+V, E, D, DV = 512, 1024, 512, 512
+FLOPS = 2 * DV * D * E
+
+F32 = mybir.dt.float32
+BF16 = mybir.dt.bfloat16
+U32 = mybir.dt.uint32
+I32 = mybir.dt.int32
+U16 = mybir.dt.uint16
+U8 = mybir.dt.uint8
+E4M3 = mybir.dt.float8_e4m3fn_x4
+E5M2 = mybir.dt.float8_e5m2_x4
+ACT = mybir.ActivationFunctionType
+ALU = mybir.AluOpType
+
+P = 128
+PACK = 4
+CHUNK = 256
+NCHUNK = E // CHUNK
+HALF = E // 2
+NODE_CHUNKS = ((0, 256), (256, 128), (384, 128))
+
+
+def tile_attend_gmp_pl_sig_ew_kernel(tc, dyT, hE, ew, wm, offs, offs2, out_0, out_1, out_2):
+    nc = tc.nc
+    with ExitStack() as ctx:
+        keep = ctx.enter_context(tc.tile_pool(name="keep", bufs=1))
+        psum = ctx.enter_context(tc.psum_pool(name="psum", bufs=1))
+
+        dst = keep.tile([P, E // 16], U16, name="dst")
+        src = keep.tile([P, E // 16], U16, name="src")
+        dy_rows = dyT.rearrange("(p t) v -> p t v", t=PACK)
+        h_rows = hE.rearrange("(p t) e -> p t e", t=PACK)
+        dy = [keep.tile([P, V], F32, name="dy%d" % t) for t in range(PACK)]
+        ews = [keep.tile([P, n], F32, name="ew%d" % s) for s, n in enumerate((CHUNK, CHUNK, HALF))]
+        hs = [[keep.tile([P, HALF], F32, name="h%d%d" % (s, t)) for t in range(PACK)] for s in range(2)]
+        w_raw = keep.tile([P, PACK, D], F32, name="w_raw")
+
+        def load_h(s, t):
+            nc.sync.dma_start(hs[s][t][:], h_rows[:, t, s * HALF : (s + 1) * HALF])
+
+        nc.sync.dma_start(dst[:], offs)
+        nc.sync.dma_start(ews[0][:], ew[:, 0:CHUNK])
+        nc.sync.dma_start(dy[0][:], dy_rows[:, 0, :])
+        load_h(0, 0)
+        nc.sync.dma_start(ews[1][:], ew[:, CHUNK:HALF])
+        for t in range(1, PACK):
+            nc.sync.dma_start(dy[t][:], dy_rows[:, t, :])
+            load_h(0, t)
+        nc.sync.dma_start(ews[2][:], ew[:, HALF:E])
+        load_h(1, 0)
+        load_h(1, 1)
+        nc.sync.dma_start(w_raw[:], wm.rearrange("(p j) d -> p j d", j=PACK))
+        load_h(1, 2)
+        load_h(1, 3)
+        nc.sync.dma_start(src[:], offs2)
+        ew_chunk = [ews[0][:], ews[1][:], ews[2][:, 0:CHUNK], ews[2][:, CHUNK:HALF]]
+
+        minus_half = keep.tile([P, 1], F32, name="minus_half")
+        nc.gpsimd.memset(minus_half[:], -0.5)
+        slope = [keep.tile([P, PACK, HALF], F32, name="slope%d" % s) for s in range(2)]
+
+        def form_slope(s, t):
+            sq = keep.tile([P, HALF], F32, name="sq%d%d" % (s, t))
+            nc.scalar.activation(sq[:], hs[s][t][:], ACT.Square, bias=minus_half[:])
+            nc.scalar.activation(slope[s][:, t, :], sq[:], ACT.Copy, bias=0.25, scale=-1.0)
+
+        for t in range(PACK):
+            form_slope(0, t)
+        form_slope(1, 0)
+        form_slope(1, 1)
+
+        w_grouped = keep.tile([P, PACK * D], BF16, name="w_grouped", tag="shared", align_bytes=64)
+        w_codes = keep.tile([P, D], U32, name="w_codes", align_bytes=64)
+        w_scales = keep.tile([P, D], U8, name="w_scales", align_bytes=64)
+        nc.scalar.copy(
+            w_grouped[:].rearrange("p (t m j) -> p m j t", t=PACK, j=PACK),
+            w_raw[:].rearrange("p j (m t) -> p m j t", t=PACK),
+        )
+        form_slope(1, 2)
+        form_slope(1, 3)
+
+        dm = [keep.tile([P, E], F32, name="dm%d" % t) for t in range(PACK)]
+        ge = []
+
+        def gather_dy(c):
+            tag = "shared" if c == NCHUNK - 1 else "ge%d" % c
+            ge.append(keep.tile([P, PACK, CHUNK], F32, name="ge%d" % c, tag=tag, align_bytes=64))
+            for t in range(PACK):
+                nc.vector.tensor_tensor(
+                    ge[c][:, t, :],
+                    dy[t][:].indirect(dst[:, c * CHUNK // 16 : (c + 1) * CHUNK // 16]),
+                    ew_chunk[c],
+                    ALU.mult,
+                )
+
+        dz_grouped = [keep.tile([P, PACK * CHUNK], BF16, name="dzg%d" % c, align_bytes=64) for c in range(NCHUNK)]
+
+        def form_dz(c):
+            s, e0 = divmod(c * CHUNK, HALF)
+            nc.vector.tensor_tensor(
+                dz_grouped[c][:].rearrange("p (g i t) -> p g t i", i=2, t=PACK),
+                ge[c][:].rearrange("p t (g i) -> p g t i", i=2),
+                slope[s][:, :, e0 : e0 + CHUNK].rearrange("p t (g i) -> p g t i", i=2),
+                ALU.mult,
+            )
+
+        def multiply(c):
+            codes = keep.tile([P, CHUNK], U32, name="dzc%d" % c, align_bytes=64)
+            scales = keep.tile([P, CHUNK], U8, name="dzs%d" % c, align_bytes=64)
+            nc.vector.quantize_mx(out=codes[:].bitcast(E5M2), scales=scales[:], in_=dz_grouped[c][:])
+            for q in range(2):
+                bank = psum.tile([P, 2, CHUNK], F32, name="bank%d%d" % (c, q))
+                for u in range(2):
+                    cols = slice((2 * q + u) * P, (2 * q + u + 1) * P)
+                    nc.tensor.matmul_mx(
+                        out=bank[:, u, :],
+                        lhsT=w_codes[:, cols].bitcast(E4M3),
+                        lhsT_scale=w_scales[:, cols],
+                        rhs=codes[:].bitcast(E5M2),
+                        rhs_scale=scales[:],
+                        start=True,
+                        stop=True,
+                    )
+                for u in range(2):
+                    target = dm[2 * q + u][:, c * CHUNK : (c + 1) * CHUNK]
+                    if c == NCHUNK - 1 and q == 0:
+                        nc.vector.tensor_copy(target, bank[:, u, :])
+                    else:
+                        nc.scalar.copy(target, bank[:, u, :])
+
+        gather_dy(0)
+        gather_dy(1)
+        gather_dy(2)
+        form_dz(0)
+        form_dz(1)
+        nc.vector.quantize_mx(out=w_codes[:].bitcast(E4M3), scales=w_scales[:], in_=w_grouped[:])
+        multiply(0)
+        multiply(1)
+        gather_dy(3)
+        form_dz(2)
+        multiply(2)
+        form_dz(3)
+        multiply(3)
+
+        out_rows = out_0.rearrange("(p t) x -> p t x", t=PACK)
+        words_out = out_1[0].rearrange("p x l -> p (x l)").bitcast(I32)
+        y_codes = keep.tile([P, V], U32, name="y_codes", align_bytes=64)
+        y_scales = keep.tile([P, V], U8, name="y_scales", align_bytes=64)
+        for k, (x0, n) in enumerate(NODE_CHUNKS):
+            picked = keep.tile([P, PACK, 2 * n], F32, name="picked%d" % k)
+            y = keep.tile([P, PACK, n], F32, name="y%d" % k)
+            entries = src[:, 2 * x0 // 16 : 2 * (x0 + n) // 16]
+            for t in range(PACK):
+                if (k == 0 and t < 2) or (k == 2 and t == 3):
+                    nc.vector.tensor_copy(picked[:, t, :], dm[t][:].indirect(entries))
+                else:
+                    nc.scalar.activation(picked[:, t, :], dm[t][:].indirect(entries), ACT.Copy)
+            pairs = picked[:].rearrange("p t (x j) -> p t x j", j=2)
+            for q in range(2):
+                nc.vector.tensor_tensor(
+                    y[:, 2 * q : 2 * q + 2, :], pairs[:, 2 * q : 2 * q + 2, :, 0], pairs[:, 2 * q : 2 * q + 2, :, 1], ALU.add
+                )
+            nc.sync.dma_start(out_rows[:, :, x0 : x0 + n], y[:])
+            y_grouped = keep.tile([P, PACK * n], BF16, name="yg%d" % k, align_bytes=64)
+            nc.vector.tensor_copy(
+                y_grouped[:].rearrange("p (g i t) -> p g t i", i=2, t=PACK),
+                y[:].rearrange("p t (g i) -> p g t i", i=2),
+            )
+            nc.vector.quantize_mx(
+                out=y_codes[:, x0 : x0 + n].bitcast(E4M3), scales=y_scales[:, x0 : x0 + n], in_=y_grouped[:]
+            )
+            nc.sync.dma_start(words_out[:, x0 : x0 + n], y_codes[:, x0 : x0 + n].bitcast(I32))
+        scales_out = out_2[0].bitcast(I32)
+        for quad in range(4):
+            queue = nc.sync if quad % 2 == 0 else nc.scalar
+            queue.dma_start(scales_out[4 * quad : 4 * quad + 4, :], y_scales[32 * quad : 32 * quad + 4, :].bitcast(I32))

@@ -18,9 +18,9 @@ ALU = mybir.AluOpType
 
 P = 128
 PACK = 4
-CHUNK = 256
-NCHUNK = E // CHUNK
 HALF = E // 2
+PIECE = 256
+EDGE_CHUNKS = ((0, 256), (256, 256), (512, 256), (768, 128), (896, 128))
 NODE_CHUNKS = ((0, 256), (256, 128), (384, 128))
 
 
@@ -35,7 +35,8 @@ def tile_attend_gmp_pl_sig_ew_kernel(tc, dyT, hE, ew, wm, offs, offs2, out_0, ou
         dy_rows = dyT.rearrange("(p t) v -> p t v", t=PACK)
         h_rows = hE.rearrange("(p t) e -> p t e", t=PACK)
         dy = [keep.tile([P, V], F32, name="dy%d" % t) for t in range(PACK)]
-        ews = [keep.tile([P, n], F32, name="ew%d" % s) for s, n in enumerate((CHUNK, CHUNK, HALF))]
+        ew_low = keep.tile([P, HALF], F32, name="ew_low")
+        ew_high = [keep.tile([P, PIECE], F32, name="ew_high%d" % s) for s in range(2)]
         hs = [[keep.tile([P, HALF], F32, name="h%d%d" % (s, t)) for t in range(PACK)] for s in range(2)]
         w_raw = keep.tile([P, PACK, D], F32, name="w_raw")
 
@@ -43,77 +44,73 @@ def tile_attend_gmp_pl_sig_ew_kernel(tc, dyT, hE, ew, wm, offs, offs2, out_0, ou
             nc.sync.dma_start(hs[s][t][:], h_rows[:, t, s * HALF : (s + 1) * HALF])
 
         nc.sync.dma_start(dst[:], offs)
-        nc.sync.dma_start(ews[0][:], ew[:, 0:CHUNK])
         nc.sync.dma_start(dy[0][:], dy_rows[:, 0, :])
-        load_h(0, 0)
-        nc.sync.dma_start(ews[1][:], ew[:, CHUNK:HALF])
+        for s in range(2):
+            nc.sync.dma_start(ew_high[s][:], ew[:, HALF + s * PIECE : HALF + (s + 1) * PIECE])
         for t in range(1, PACK):
             nc.sync.dma_start(dy[t][:], dy_rows[:, t, :])
-            load_h(0, t)
-        nc.sync.dma_start(ews[2][:], ew[:, HALF:E])
-        load_h(1, 0)
-        load_h(1, 1)
+        load_h(0, 0)
         nc.sync.dma_start(w_raw[:], wm.rearrange("(p j) d -> p j d", j=PACK))
-        load_h(1, 2)
-        load_h(1, 3)
+        for t in range(1, PACK):
+            load_h(0, t)
+        nc.sync.dma_start(ew_low[:], ew[:, 0:HALF])
+        for t in range(PACK):
+            load_h(1, t)
         nc.sync.dma_start(src[:], offs2)
-        ew_chunk = [ews[0][:], ews[1][:], ews[2][:, 0:CHUNK], ews[2][:, CHUNK:HALF]]
 
         minus_half = keep.tile([P, 1], F32, name="minus_half")
         nc.gpsimd.memset(minus_half[:], -0.5)
-        slope = [keep.tile([P, PACK, HALF], F32, name="slope%d" % s) for s in range(2)]
 
-        def form_slope(s, t):
-            sq = keep.tile([P, HALF], F32, name="sq%d%d" % (s, t))
-            nc.scalar.activation(sq[:], hs[s][t][:], ACT.Square, bias=minus_half[:])
-            nc.scalar.activation(slope[s][:, t, :], sq[:], ACT.Copy, bias=0.25, scale=-1.0)
-
+        looked = [keep.tile([P, PACK, HALF], F32, name="looked%d" % s) for s in range(2)]
         for t in range(PACK):
-            form_slope(0, t)
-        form_slope(1, 0)
-        form_slope(1, 1)
+            for s in range(2):
+                cols = slice(s * PIECE, (s + 1) * PIECE)
+                low = dst[:, s * PIECE // 16 : (s + 1) * PIECE // 16]
+                high = dst[:, (HALF + s * PIECE) // 16 : (HALF + (s + 1) * PIECE) // 16]
+                nc.scalar.activation(looked[0][:, t, cols], dy[t][:].indirect(low), ACT.Copy, scale=-1.0)
+                nc.vector.tensor_tensor(looked[1][:, t, cols], dy[t][:].indirect(high), ew_high[s][:], ALU.mult)
 
-        w_grouped = keep.tile([P, PACK * D], BF16, name="w_grouped", tag="shared", align_bytes=64)
+        w_grouped = keep.tile([P, PACK * D], BF16, name="w_grouped", align_bytes=64)
         w_codes = keep.tile([P, D], U32, name="w_codes", align_bytes=64)
         w_scales = keep.tile([P, D], U8, name="w_scales", align_bytes=64)
-        nc.scalar.copy(
+        nc.vector.tensor_copy(
             w_grouped[:].rearrange("p (t m j) -> p m j t", t=PACK, j=PACK),
             w_raw[:].rearrange("p j (m t) -> p m j t", t=PACK),
         )
-        form_slope(1, 2)
-        form_slope(1, 3)
+        nc.vector.quantize_mx(out=w_codes[:].bitcast(E4M3), scales=w_scales[:], in_=w_grouped[:])
+
+        factor = [keep.tile([P, PACK, HALF], F32, name="factor%d" % s) for s in range(2)]
+        for s in range(2):
+            for t in range(PACK):
+                sq = keep.tile([P, HALF], F32, name="sq%d%d" % (s, t))
+                nc.scalar.activation(sq[:], hs[s][t][:], ACT.Square, bias=minus_half[:])
+                if s == 0:
+                    nc.vector.scalar_tensor_tensor(factor[s][:, t, :], sq[:], 0.25, ew_low[:], ALU.subtract, ALU.mult)
+                else:
+                    nc.scalar.activation(factor[s][:, t, :], sq[:], ACT.Copy, bias=0.25, scale=-1.0)
 
         dm = [keep.tile([P, E], F32, name="dm%d" % t) for t in range(PACK)]
-        ge = []
-
-        def gather_dy(c):
-            tag = "shared" if c == NCHUNK - 1 else "ge%d" % c
-            ge.append(keep.tile([P, PACK, CHUNK], F32, name="ge%d" % c, tag=tag, align_bytes=64))
-            for t in range(PACK):
-                nc.vector.tensor_tensor(
-                    ge[c][:, t, :],
-                    dy[t][:].indirect(dst[:, c * CHUNK // 16 : (c + 1) * CHUNK // 16]),
-                    ew_chunk[c],
-                    ALU.mult,
-                )
-
-        dz_grouped = [keep.tile([P, PACK * CHUNK], BF16, name="dzg%d" % c, align_bytes=64) for c in range(NCHUNK)]
+        dz_grouped = [
+            keep.tile([P, PACK * n], BF16, name="dzg%d" % c, align_bytes=64) for c, (e0, n) in enumerate(EDGE_CHUNKS)
+        ]
 
         def form_dz(c):
-            s, e0 = divmod(c * CHUNK, HALF)
+            e0, n = EDGE_CHUNKS[c]
+            s, a = divmod(e0, HALF)
             nc.vector.tensor_tensor(
                 dz_grouped[c][:].rearrange("p (g i t) -> p g t i", i=2, t=PACK),
-                ge[c][:].rearrange("p t (g i) -> p g t i", i=2),
-                slope[s][:, :, e0 : e0 + CHUNK].rearrange("p t (g i) -> p g t i", i=2),
+                looked[s][:, :, a : a + n].rearrange("p t (g i) -> p g t i", i=2),
+                factor[s][:, :, a : a + n].rearrange("p t (g i) -> p g t i", i=2),
                 ALU.mult,
             )
 
         def multiply(c):
-            codes = keep.tile([P, CHUNK], U32, name="dzc%d" % c, align_bytes=64)
-            scales = keep.tile([P, CHUNK], U8, name="dzs%d" % c, align_bytes=64)
+            e0, n = EDGE_CHUNKS[c]
+            codes = keep.tile([P, n], U32, name="dzc%d" % c, align_bytes=64)
+            scales = keep.tile([P, n], U8, name="dzs%d" % c, align_bytes=64)
             nc.vector.quantize_mx(out=codes[:].bitcast(E5M2), scales=scales[:], in_=dz_grouped[c][:])
             for q in range(2):
-                bank = psum.tile([P, 2, CHUNK], F32, name="bank%d%d" % (c, q))
+                bank = psum.tile([P, 2, n], F32, name="bank%d%d" % (c, q), tag="bank%d%d" % (c % 4, q))
                 for u in range(2):
                     cols = slice((2 * q + u) * P, (2 * q + u + 1) * P)
                     nc.tensor.matmul_mx(
@@ -126,25 +123,17 @@ def tile_attend_gmp_pl_sig_ew_kernel(tc, dyT, hE, ew, wm, offs, offs2, out_0, ou
                         stop=True,
                     )
                 for u in range(2):
-                    target = dm[2 * q + u][:, c * CHUNK : (c + 1) * CHUNK]
-                    if c == NCHUNK - 1 and q == 0:
+                    target = dm[2 * q + u][:, e0 : e0 + n]
+                    if c >= 2 and q == 0:
                         nc.vector.tensor_copy(target, bank[:, u, :])
                     else:
                         nc.scalar.copy(target, bank[:, u, :])
 
-        gather_dy(0)
-        gather_dy(1)
-        gather_dy(2)
         form_dz(0)
-        form_dz(1)
-        nc.vector.quantize_mx(out=w_codes[:].bitcast(E4M3), scales=w_scales[:], in_=w_grouped[:])
-        multiply(0)
-        multiply(1)
-        gather_dy(3)
-        form_dz(2)
-        multiply(2)
-        form_dz(3)
-        multiply(3)
+        for c in range(1, len(EDGE_CHUNKS)):
+            form_dz(c)
+            multiply(c - 1)
+        multiply(len(EDGE_CHUNKS) - 1)
 
         out_rows = out_0.rearrange("(p t) x -> p t x", t=PACK)
         words_out = out_1[0].rearrange("p x l -> p (x l)").bitcast(I32)
@@ -154,8 +143,8 @@ def tile_attend_gmp_pl_sig_ew_kernel(tc, dyT, hE, ew, wm, offs, offs2, out_0, ou
             picked = keep.tile([P, PACK, 2 * n], F32, name="picked%d" % k)
             y = keep.tile([P, PACK, n], F32, name="y%d" % k)
             entries = src[:, 2 * x0 // 16 : 2 * (x0 + n) // 16]
-            for t in range(PACK):
-                if (k == 0 and t < 2) or (k == 2 and t == 3):
+            for t in (0, 2, 1, 3):
+                if t == 0 or (k == 0 and t == 1):
                     nc.vector.tensor_copy(picked[:, t, :], dm[t][:].indirect(entries))
                 else:
                     nc.scalar.activation(picked[:, t, :], dm[t][:].indirect(entries), ACT.Copy)

@@ -1,6 +1,7 @@
 from contextlib import ExitStack
 
 import concourse.mybir as mybir
+from concourse.masks import make_identity
 
 V, E, D, DV = 512, 1024, 512, 512
 FLOPS = 2 * DV * D * E
@@ -18,9 +19,11 @@ ALU = mybir.AluOpType
 
 P = 128
 PACK = 4
-HALF = E // 2
-PIECE = 256
-EDGE_CHUNKS = ((0, 256), (256, 256), (512, 256), (768, 128), (896, 128))
+LOW = 384
+HIGH = E - LOW
+PIECE = HIGH // 2
+SPREAD = LOW // P
+EDGE_CHUNKS = ((0, 256), (256, 128), (384, 256), (640, 256), (896, 128))
 NODE_CHUNKS = ((0, 256), (256, 128), (384, 128))
 
 
@@ -35,68 +38,74 @@ def tile_attend_gmp_pl_sig_ew_kernel(tc, dyT, hE, ew, wm, offs, offs2, out_0, ou
         dy_rows = dyT.rearrange("(p t) v -> p t v", t=PACK)
         h_rows = hE.rearrange("(p t) e -> p t e", t=PACK)
         dy = [keep.tile([P, V], F32, name="dy%d" % t) for t in range(PACK)]
-        ew_low = keep.tile([P, HALF], F32, name="ew_low")
+        ew_column = keep.tile([P, SPREAD], F32, name="ew_column")
         ew_high = [keep.tile([P, PIECE], F32, name="ew_high%d" % s) for s in range(2)]
-        hs = [[keep.tile([P, HALF], F32, name="h%d%d" % (s, t)) for t in range(PACK)] for s in range(2)]
+        h_low = [keep.tile([P, LOW], F32, name="h_low%d" % t) for t in range(PACK)]
+        h_high = [keep.tile([P, 2, HIGH], F32, name="h_high%d" % q) for q in range(2)]
         w_raw = keep.tile([P, PACK, D], F32, name="w_raw")
-
-        def load_h(s, t):
-            nc.sync.dma_start(hs[s][t][:], h_rows[:, t, s * HALF : (s + 1) * HALF])
 
         nc.sync.dma_start(dst[:], offs)
         nc.sync.dma_start(dy[0][:], dy_rows[:, 0, :])
         for s in range(2):
-            nc.sync.dma_start(ew_high[s][:], ew[:, HALF + s * PIECE : HALF + (s + 1) * PIECE])
-        for t in range(1, PACK):
-            nc.sync.dma_start(dy[t][:], dy_rows[:, t, :])
-        load_h(0, 0)
-        nc.sync.dma_start(w_raw[:], wm.rearrange("(p j) d -> p j d", j=PACK))
-        for t in range(1, PACK):
-            load_h(0, t)
-        nc.sync.dma_start(ew_low[:], ew[:, 0:HALF])
+            nc.sync.dma_start(ew_high[s][:], ew[:, LOW + s * PIECE : LOW + (s + 1) * PIECE])
+        nc.sync.dma_start(dy[1][:], dy_rows[:, 1, :])
+        nc.sync.dma_start(dy[2][:], dy_rows[:, 2, :])
+        nc.sync.dma_start(ew_column[:], ew[0, 0:LOW].rearrange("(k c) -> k c", c=SPREAD))
+        nc.sync.dma_start(dy[3][:], dy_rows[:, 3, :])
         for t in range(PACK):
-            load_h(1, t)
+            nc.sync.dma_start(h_low[t][:], h_rows[:, t, 0:LOW])
+        nc.sync.dma_start(h_high[0][:], h_rows[:, 0:2, LOW:E])
+        nc.sync.dma_start(h_high[1][:], h_rows[:, 2:4, LOW:E])
+        nc.sync.dma_start(w_raw[:], wm.rearrange("(p j) d -> p j d", j=PACK))
         nc.sync.dma_start(src[:], offs2)
+
+        identity = keep.tile([P, P], F32, name="identity")
+        make_identity(nc, identity[:])
+        ew_low = psum.tile([P, SPREAD, P], F32, name="ew_low", tag="bank7")
+        for c in range(SPREAD):
+            nc.tensor.transpose(ew_low[:, c, :], ew_column[:, c : c + 1].to_broadcast([P, P]), identity[:])
 
         minus_half = keep.tile([P, 1], F32, name="minus_half")
         nc.gpsimd.memset(minus_half[:], -0.5)
 
-        looked = [keep.tile([P, PACK, HALF], F32, name="looked%d" % s) for s in range(2)]
+        looked = [keep.tile([P, PACK, n], F32, name="looked%d" % s) for s, n in enumerate((LOW, HIGH))]
         for t in range(PACK):
+            nc.scalar.activation(looked[0][:, t, :], dy[t][:].indirect(dst[:, 0 : LOW // 16]), ACT.Copy, scale=-1.0)
             for s in range(2):
-                cols = slice(s * PIECE, (s + 1) * PIECE)
-                low = dst[:, s * PIECE // 16 : (s + 1) * PIECE // 16]
-                high = dst[:, (HALF + s * PIECE) // 16 : (HALF + (s + 1) * PIECE) // 16]
-                nc.scalar.activation(looked[0][:, t, cols], dy[t][:].indirect(low), ACT.Copy, scale=-1.0)
-                nc.vector.tensor_tensor(looked[1][:, t, cols], dy[t][:].indirect(high), ew_high[s][:], ALU.mult)
+                high = dst[:, (LOW + s * PIECE) // 16 : (LOW + (s + 1) * PIECE) // 16]
+                nc.vector.tensor_tensor(
+                    looked[1][:, t, s * PIECE : (s + 1) * PIECE], dy[t][:].indirect(high), ew_high[s][:], ALU.mult
+                )
 
-        w_grouped = keep.tile([P, PACK * D], BF16, name="w_grouped", align_bytes=64)
+        w_grouped = keep.tile([P, PACK * D], BF16, name="w_grouped", tag="grouped1", align_bytes=64)
         w_codes = keep.tile([P, D], U32, name="w_codes", align_bytes=64)
         w_scales = keep.tile([P, D], U8, name="w_scales", align_bytes=64)
-        nc.vector.tensor_copy(
-            w_grouped[:].rearrange("p (t m j) -> p m j t", t=PACK, j=PACK),
-            w_raw[:].rearrange("p j (m t) -> p m j t", t=PACK),
-        )
-        nc.vector.quantize_mx(out=w_codes[:].bitcast(E4M3), scales=w_scales[:], in_=w_grouped[:])
 
-        factor = [keep.tile([P, PACK, HALF], F32, name="factor%d" % s) for s in range(2)]
-        for s in range(2):
-            for t in range(PACK):
-                sq = keep.tile([P, HALF], F32, name="sq%d%d" % (s, t))
-                nc.scalar.activation(sq[:], hs[s][t][:], ACT.Square, bias=minus_half[:])
-                if s == 0:
-                    nc.vector.scalar_tensor_tensor(factor[s][:, t, :], sq[:], 0.25, ew_low[:], ALU.subtract, ALU.mult)
-                else:
-                    nc.scalar.activation(factor[s][:, t, :], sq[:], ACT.Copy, bias=0.25, scale=-1.0)
+        factor = [keep.tile([P, PACK, n], F32, name="factor%d" % s) for s, n in enumerate((LOW, HIGH))]
+        for t in range(PACK):
+            sq = keep.tile([P, LOW], F32, name="sq_low%d" % t)
+            nc.scalar.activation(sq[:], h_low[t][:], ACT.Square, bias=minus_half[:])
+            nc.vector.scalar_tensor_tensor(
+                factor[0][:, t, :].rearrange("p (k c) -> p k c", c=SPREAD),
+                sq[:].rearrange("p (k c) -> p k c", c=SPREAD),
+                0.25,
+                ew_low[:].rearrange("p c k -> p k c"),
+                ALU.subtract,
+                ALU.mult,
+            )
+        for q in range(2):
+            sq = keep.tile([P, 2, HIGH], F32, name="sq_high%d" % q)
+            nc.scalar.activation(sq[:], h_high[q][:], ACT.Square, bias=minus_half[:])
+            nc.scalar.activation(factor[1][:, 2 * q : 2 * q + 2, :], sq[:], ACT.Copy, bias=0.25, scale=-1.0)
 
-        dm = [keep.tile([P, E], F32, name="dm%d" % t) for t in range(PACK)]
-        dz_grouped = [
-            keep.tile([P, PACK * n], BF16, name="dzg%d" % c, align_bytes=64) for c, (e0, n) in enumerate(EDGE_CHUNKS)
-        ]
+        dm = keep.tile([P, PACK, E], F32, name="dm")
+        dz_grouped = []
+        late_copies = []
 
         def form_dz(c):
             e0, n = EDGE_CHUNKS[c]
-            s, a = divmod(e0, HALF)
+            s, a = (0, e0) if e0 < LOW else (1, e0 - LOW)
+            dz_grouped.append(keep.tile([P, PACK * n], BF16, name="dzg%d" % c, tag="grouped%d" % c, align_bytes=64))
             nc.vector.tensor_tensor(
                 dz_grouped[c][:].rearrange("p (g i t) -> p g t i", i=2, t=PACK),
                 looked[s][:, :, a : a + n].rearrange("p t (g i) -> p g t i", i=2),
@@ -110,7 +119,7 @@ def tile_attend_gmp_pl_sig_ew_kernel(tc, dyT, hE, ew, wm, offs, offs2, out_0, ou
             scales = keep.tile([P, n], U8, name="dzs%d" % c, align_bytes=64)
             nc.vector.quantize_mx(out=codes[:].bitcast(E5M2), scales=scales[:], in_=dz_grouped[c][:])
             for q in range(2):
-                bank = psum.tile([P, 2, n], F32, name="bank%d%d" % (c, q), tag="bank%d%d" % (c % 4, q))
+                bank = psum.tile([P, 2, n], F32, name="bank%d%d" % (c, q), tag="bank%d" % ((2 * c + q) % 8))
                 for u in range(2):
                     cols = slice((2 * q + u) * P, (2 * q + u + 1) * P)
                     nc.tensor.matmul_mx(
@@ -122,18 +131,24 @@ def tile_attend_gmp_pl_sig_ew_kernel(tc, dyT, hE, ew, wm, offs, offs2, out_0, ou
                         start=True,
                         stop=True,
                     )
-                for u in range(2):
-                    target = dm[2 * q + u][:, e0 : e0 + n]
-                    if c >= 2 and q == 0:
-                        nc.vector.tensor_copy(target, bank[:, u, :])
-                    else:
-                        nc.scalar.copy(target, bank[:, u, :])
+                target = dm[:, 2 * q : 2 * q + 2, e0 : e0 + n]
+                if c >= 3 and q == 0:
+                    late_copies.append((target, bank[:]))
+                else:
+                    nc.scalar.copy(target, bank[:])
 
         form_dz(0)
+        w_to = w_grouped[:].rearrange("p (t m j) -> p m j t", t=PACK, j=PACK)
+        w_from = w_raw[:].rearrange("p j (m t) -> p m j t", t=PACK)
+        nc.vector.tensor_copy(w_to, w_from)
+        nc.vector.quantize_mx(out=w_codes[:].bitcast(E4M3), scales=w_scales[:], in_=w_grouped[:])
+
         for c in range(1, len(EDGE_CHUNKS)):
             form_dz(c)
             multiply(c - 1)
         multiply(len(EDGE_CHUNKS) - 1)
+        for target, source in late_copies:
+            nc.vector.tensor_copy(target, source)
 
         out_rows = out_0.rearrange("(p t) x -> p t x", t=PACK)
         words_out = out_1[0].rearrange("p x l -> p (x l)").bitcast(I32)
@@ -145,9 +160,9 @@ def tile_attend_gmp_pl_sig_ew_kernel(tc, dyT, hE, ew, wm, offs, offs2, out_0, ou
             entries = src[:, 2 * x0 // 16 : 2 * (x0 + n) // 16]
             for t in (0, 2, 1, 3):
                 if t == 0 or (k == 0 and t == 1):
-                    nc.vector.tensor_copy(picked[:, t, :], dm[t][:].indirect(entries))
+                    nc.vector.tensor_copy(picked[:, t, :], dm[:, t, :].indirect(entries))
                 else:
-                    nc.scalar.activation(picked[:, t, :], dm[t][:].indirect(entries), ACT.Copy)
+                    nc.scalar.activation(picked[:, t, :], dm[:, t, :].indirect(entries), ACT.Copy)
             pairs = picked[:].rearrange("p t (x j) -> p t x j", j=2)
             for q in range(2):
                 nc.vector.tensor_tensor(

@@ -23,7 +23,8 @@ LOW = 384
 HIGH = E - LOW
 PIECE = HIGH // 2
 SPREAD = LOW // P
-EDGE_CHUNKS = ((0, 256), (256, 128), (384, 256), (640, 256), (896, 128))
+EDGE_CHUNKS = ((0, 256), (256, 128), (384, 256), (640, 128), (768, 128), (896, 128))
+PLANE_CHUNKS = ((0, 256), (256, 384), (384, 512))
 NODE_CHUNKS = ((0, 256), (256, 128), (384, 128))
 
 
@@ -94,13 +95,14 @@ def tile_attend_gmp_pl_sig_ew_kernel(tc, dyT, hE, ew, wm, offs, offs2, out_0, ou
                 ALU.mult,
             )
         for q in range(2):
-            sq = keep.tile([P, 2, HIGH], F32, name="sq_high%d" % q)
+            sq = keep.tile([P, 2, HIGH], F32, name="sq_high%d" % q, tag="squares%d" % q)
             nc.scalar.activation(sq[:], h_high[q][:], ACT.Square, bias=minus_half[:])
             nc.scalar.activation(factor[1][:, 2 * q : 2 * q + 2, :], sq[:], ACT.Copy, bias=0.25, scale=-1.0)
 
-        dm = keep.tile([P, PACK, E], F32, name="dm")
+        dm = keep.tile([P, PACK, E], F32, name="dm", tag="squares1")
         dz_grouped = []
         late_copies = []
+        banks = []
 
         def form_dz(c):
             e0, n = EDGE_CHUNKS[c]
@@ -118,10 +120,12 @@ def tile_attend_gmp_pl_sig_ew_kernel(tc, dyT, hE, ew, wm, offs, offs2, out_0, ou
             codes = keep.tile([P, n], U32, name="dzc%d" % c, align_bytes=64)
             scales = keep.tile([P, n], U8, name="dzs%d" % c, align_bytes=64)
             nc.vector.quantize_mx(out=codes[:].bitcast(E5M2), scales=scales[:], in_=dz_grouped[c][:])
-            for q in range(2):
-                bank = psum.tile([P, 2, n], F32, name="bank%d%d" % (c, q), tag="bank%d" % ((2 * c + q) % 8))
-                for u in range(2):
-                    cols = slice((2 * q + u) * P, (2 * q + u + 1) * P)
+            per_bank = 2 if n > P or c == len(EDGE_CHUNKS) - 1 else PACK
+            for t0 in range(0, PACK, per_bank):
+                bank = psum.tile([P, per_bank, n], F32, name="bank%d%d" % (c, t0), tag="bank%d" % (len(banks) % 8))
+                banks.append(bank)
+                for u in range(per_bank):
+                    cols = slice((t0 + u) * P, (t0 + u + 1) * P)
                     nc.tensor.matmul_mx(
                         out=bank[:, u, :],
                         lhsT=w_codes[:, cols].bitcast(E4M3),
@@ -131,8 +135,8 @@ def tile_attend_gmp_pl_sig_ew_kernel(tc, dyT, hE, ew, wm, offs, offs2, out_0, ou
                         start=True,
                         stop=True,
                     )
-                target = dm[:, 2 * q : 2 * q + 2, e0 : e0 + n]
-                if c >= 3 and q == 0:
+                target = dm[:, t0 : t0 + per_bank, e0 : e0 + n]
+                if c >= 4 and t0 == 0:
                     late_copies.append((target, bank[:]))
                 else:
                     nc.scalar.copy(target, bank[:])
@@ -154,12 +158,13 @@ def tile_attend_gmp_pl_sig_ew_kernel(tc, dyT, hE, ew, wm, offs, offs2, out_0, ou
         words_out = out_1[0].rearrange("p x l -> p (x l)").bitcast(I32)
         y_codes = keep.tile([P, V], U32, name="y_codes", align_bytes=64)
         y_scales = keep.tile([P, V], U8, name="y_scales", align_bytes=64)
+        y_grouped = keep.tile([P, PACK * V], BF16, name="y_grouped", align_bytes=64)
         for k, (x0, n) in enumerate(NODE_CHUNKS):
             picked = keep.tile([P, PACK, 2 * n], F32, name="picked%d" % k)
             y = keep.tile([P, PACK, n], F32, name="y%d" % k)
             entries = src[:, 2 * x0 // 16 : 2 * (x0 + n) // 16]
             for t in (0, 2, 1, 3):
-                if t == 0 or (k == 0 and t == 1):
+                if (k == 0 and t < 2) or (k == 2 and t == 0):
                     nc.vector.tensor_copy(picked[:, t, :], dm[:, t, :].indirect(entries))
                 else:
                     nc.scalar.activation(picked[:, t, :], dm[:, t, :].indirect(entries), ACT.Copy)
@@ -169,15 +174,16 @@ def tile_attend_gmp_pl_sig_ew_kernel(tc, dyT, hE, ew, wm, offs, offs2, out_0, ou
                     y[:, 2 * q : 2 * q + 2, :], pairs[:, 2 * q : 2 * q + 2, :, 0], pairs[:, 2 * q : 2 * q + 2, :, 1], ALU.add
                 )
             nc.sync.dma_start(out_rows[:, :, x0 : x0 + n], y[:])
-            y_grouped = keep.tile([P, PACK * n], BF16, name="yg%d" % k, align_bytes=64)
             nc.vector.tensor_copy(
-                y_grouped[:].rearrange("p (g i t) -> p g t i", i=2, t=PACK),
+                y_grouped[:, PACK * x0 : PACK * (x0 + n)].rearrange("p (g i t) -> p g t i", i=2, t=PACK),
                 y[:].rearrange("p t (g i) -> p g t i", i=2),
             )
-            nc.vector.quantize_mx(
-                out=y_codes[:, x0 : x0 + n].bitcast(E4M3), scales=y_scales[:, x0 : x0 + n], in_=y_grouped[:]
-            )
-            nc.sync.dma_start(words_out[:, x0 : x0 + n], y_codes[:, x0 : x0 + n].bitcast(I32))
+            for a, b in PLANE_CHUNKS:
+                if x0 < b <= x0 + n:
+                    nc.vector.quantize_mx(
+                        out=y_codes[:, a:b].bitcast(E4M3), scales=y_scales[:, a:b], in_=y_grouped[:, PACK * a : PACK * b]
+                    )
+                    nc.sync.dma_start(words_out[:, a:b], y_codes[:, a:b].bitcast(I32))
         scales_out = out_2[0].bitcast(I32)
         for quad in range(4):
             queue = nc.sync if quad % 2 == 0 else nc.scalar

@@ -21,11 +21,12 @@ P = 128
 PACK = 4
 LOW = 384
 HIGH = E - LOW
-PIECE = HIGH // 2
+PIECES = ((384, 192), (576, 448))
 SPREAD = LOW // P
+HIGH_PLANES = ((0, 2), (2, 3), (3, 4))
 EDGE_CHUNKS = ((0, 256), (256, 128), (384, 256), (640, 128), (768, 128), (896, 128))
 PLANE_CHUNKS = ((0, 256), (256, 384), (384, 512))
-NODE_CHUNKS = ((0, 256), (256, 128), (384, 128))
+NODE_CHUNKS = ((0, 256), (256, 192), (448, 64))
 
 
 def tile_attend_gmp_pl_sig_ew_kernel(tc, dyT, hE, ew, wm, offs, offs2, out_0, out_1, out_2):
@@ -40,15 +41,15 @@ def tile_attend_gmp_pl_sig_ew_kernel(tc, dyT, hE, ew, wm, offs, offs2, out_0, ou
         h_rows = hE.rearrange("(p t) e -> p t e", t=PACK)
         dy = [keep.tile([P, V], F32, name="dy%d" % t) for t in range(PACK)]
         ew_column = keep.tile([P, SPREAD], F32, name="ew_column")
-        ew_high = [keep.tile([P, PIECE], F32, name="ew_high%d" % s) for s in range(2)]
+        ew_high = [keep.tile([P, n], F32, name="ew_high%d" % s) for s, (e0, n) in enumerate(PIECES)]
         h_low = [keep.tile([P, LOW], F32, name="h_low%d" % t) for t in range(PACK)]
-        h_high = [keep.tile([P, 2, HIGH], F32, name="h_high%d" % q) for q in range(2)]
+        h_high = [keep.tile([P, b - a, HIGH], F32, name="h_high%d" % a) for a, b in HIGH_PLANES]
         w_raw = keep.tile([P, PACK, D], F32, name="w_raw")
 
-        nc.sync.dma_start(dst[:], offs)
         nc.sync.dma_start(dy[0][:], dy_rows[:, 0, :])
-        for s in range(2):
-            nc.sync.dma_start(ew_high[s][:], ew[:, LOW + s * PIECE : LOW + (s + 1) * PIECE])
+        nc.sync.dma_start(dst[:], offs)
+        for s, (e0, n) in enumerate(PIECES):
+            nc.sync.dma_start(ew_high[s][:], ew[:, e0 : e0 + n])
         nc.sync.dma_start(dy[1][:], dy_rows[:, 1, :])
         nc.sync.dma_start(dy[2][:], dy_rows[:, 2, :])
         nc.sync.dma_start(ew_column[:], ew[0, 0:LOW].rearrange("(k c) -> k c", c=SPREAD))
@@ -56,8 +57,9 @@ def tile_attend_gmp_pl_sig_ew_kernel(tc, dyT, hE, ew, wm, offs, offs2, out_0, ou
         for t in range(PACK):
             nc.sync.dma_start(h_low[t][:], h_rows[:, t, 0:LOW])
         nc.sync.dma_start(h_high[0][:], h_rows[:, 0:2, LOW:E])
-        nc.sync.dma_start(h_high[1][:], h_rows[:, 2:4, LOW:E])
+        nc.sync.dma_start(h_high[1][:], h_rows[:, 2:3, LOW:E])
         nc.sync.dma_start(w_raw[:], wm.rearrange("(p j) d -> p j d", j=PACK))
+        nc.sync.dma_start(h_high[2][:], h_rows[:, 3:4, LOW:E])
         nc.sync.dma_start(src[:], offs2)
 
         identity = keep.tile([P, P], F32, name="identity")
@@ -72,10 +74,10 @@ def tile_attend_gmp_pl_sig_ew_kernel(tc, dyT, hE, ew, wm, offs, offs2, out_0, ou
         looked = [keep.tile([P, PACK, n], F32, name="looked%d" % s) for s, n in enumerate((LOW, HIGH))]
         for t in range(PACK):
             nc.scalar.activation(looked[0][:, t, :], dy[t][:].indirect(dst[:, 0 : LOW // 16]), ACT.Copy, scale=-1.0)
-            for s in range(2):
-                high = dst[:, (LOW + s * PIECE) // 16 : (LOW + (s + 1) * PIECE) // 16]
+            for s, (e0, n) in enumerate(PIECES):
+                high = dst[:, e0 // 16 : (e0 + n) // 16]
                 nc.vector.tensor_tensor(
-                    looked[1][:, t, s * PIECE : (s + 1) * PIECE], dy[t][:].indirect(high), ew_high[s][:], ALU.mult
+                    looked[1][:, t, e0 - LOW : e0 - LOW + n], dy[t][:].indirect(high), ew_high[s][:], ALU.mult
                 )
 
         w_grouped = keep.tile([P, PACK * D], BF16, name="w_grouped", tag="grouped1", align_bytes=64)
@@ -94,12 +96,12 @@ def tile_attend_gmp_pl_sig_ew_kernel(tc, dyT, hE, ew, wm, offs, offs2, out_0, ou
                 ALU.subtract,
                 ALU.mult,
             )
-        for q in range(2):
-            sq = keep.tile([P, 2, HIGH], F32, name="sq_high%d" % q, tag="squares%d" % q)
+        for q, (a, b) in enumerate(HIGH_PLANES):
+            sq = keep.tile([P, b - a, HIGH], F32, name="sq_high%d" % q, tag="squares%d" % q)
             nc.scalar.activation(sq[:], h_high[q][:], ACT.Square, bias=minus_half[:])
-            nc.scalar.activation(factor[1][:, 2 * q : 2 * q + 2, :], sq[:], ACT.Copy, bias=0.25, scale=-1.0)
+            nc.scalar.activation(factor[1][:, a:b, :], sq[:], ACT.Copy, bias=0.25, scale=-1.0)
 
-        dm = keep.tile([P, PACK, E], F32, name="dm", tag="squares1")
+        dm = keep.tile([P, PACK, E], F32, name="dm", tag="squares2")
         dz_grouped = []
         late_copies = []
         banks = []
@@ -164,7 +166,7 @@ def tile_attend_gmp_pl_sig_ew_kernel(tc, dyT, hE, ew, wm, offs, offs2, out_0, ou
             y = keep.tile([P, PACK, n], F32, name="y%d" % k)
             entries = src[:, 2 * x0 // 16 : 2 * (x0 + n) // 16]
             for t in (0, 2, 1, 3):
-                if (k == 0 and t < 2) or (k == 2 and t == 0):
+                if (k == 0 and t < 2) or (k == 2 and t < 2):
                     nc.vector.tensor_copy(picked[:, t, :], dm[:, t, :].indirect(entries))
                 else:
                     nc.scalar.activation(picked[:, t, :], dm[:, t, :].indirect(entries), ACT.Copy)
@@ -183,7 +185,7 @@ def tile_attend_gmp_pl_sig_ew_kernel(tc, dyT, hE, ew, wm, offs, offs2, out_0, ou
                     nc.vector.quantize_mx(
                         out=y_codes[:, a:b].bitcast(E4M3), scales=y_scales[:, a:b], in_=y_grouped[:, PACK * a : PACK * b]
                     )
-                    nc.sync.dma_start(words_out[:, a:b], y_codes[:, a:b].bitcast(I32))
+                    (nc.scalar if b == V else nc.sync).dma_start(words_out[:, a:b], y_codes[:, a:b].bitcast(I32))
         scales_out = out_2[0].bitcast(I32)
         for quad in range(4):
             queue = nc.sync if quad % 2 == 0 else nc.scalar

from contextlib import ExitStack

import concourse.mybir as mybir
from concourse.masks import make_identity

V, E, D, DV = 512, 1024, 512, 512
FLOPS = 2 * DV * D * E

F32 = mybir.dt.float32
BF16 = mybir.dt.bfloat16
U32 = mybir.dt.uint32
I32 = mybir.dt.int32
U16 = mybir.dt.uint16
U8 = mybir.dt.uint8
E4M3 = mybir.dt.float8_e4m3fn_x4
E5M2 = mybir.dt.float8_e5m2_x4
ACT = mybir.ActivationFunctionType
ALU = mybir.AluOpType

P = 128
PACK = 4
LOW = 384
HIGH = E - LOW
PIECES = ((384, 192), (576, 448))
SPREAD = LOW // P
HIGH_PLANES = ((0, 2), (2, 3), (3, 4))
EDGE_CHUNKS = ((0, 256), (256, 128), (384, 256), (640, 128), (768, 128), (896, 128))
PLANE_CHUNKS = ((0, 256), (256, 384), (384, 512))
NODE_CHUNKS = ((0, 256), (256, 192), (448, 64))


def tile_attend_gmp_pl_sig_ew_kernel(tc, dyT, hE, ew, wm, offs, offs2, out_0, out_1, out_2):
    nc = tc.nc
    with ExitStack() as ctx:
        keep = ctx.enter_context(tc.tile_pool(name="keep", bufs=1))
        psum = ctx.enter_context(tc.psum_pool(name="psum", bufs=1))

        dst = keep.tile([P, E // 16], U16, name="dst")
        src = keep.tile([P, E // 16], U16, name="src")
        dy_rows = dyT.rearrange("(p t) v -> p t v", t=PACK)
        h_rows = hE.rearrange("(p t) e -> p t e", t=PACK)
        dy = [keep.tile([P, V], F32, name="dy%d" % t) for t in range(PACK)]
        ew_column = keep.tile([P, SPREAD], F32, name="ew_column")
        ew_high = [keep.tile([P, n], F32, name="ew_high%d" % s) for s, (e0, n) in enumerate(PIECES)]
        h_low = [keep.tile([P, LOW], F32, name="h_low%d" % t) for t in range(PACK)]
        h_high = [keep.tile([P, b - a, HIGH], F32, name="h_high%d" % a) for a, b in HIGH_PLANES]
        w_raw = keep.tile([P, PACK, D], F32, name="w_raw")

        nc.sync.dma_start(dy[0][:], dy_rows[:, 0, :])
        nc.sync.dma_start(dst[:], offs)
        for s, (e0, n) in enumerate(PIECES):
            nc.sync.dma_start(ew_high[s][:], ew[:, e0 : e0 + n])
        nc.sync.dma_start(dy[1][:], dy_rows[:, 1, :])
        nc.sync.dma_start(dy[2][:], dy_rows[:, 2, :])
        nc.sync.dma_start(ew_column[:], ew[0, 0:LOW].rearrange("(k c) -> k c", c=SPREAD))
        nc.sync.dma_start(dy[3][:], dy_rows[:, 3, :])
        for t in range(PACK):
            nc.sync.dma_start(h_low[t][:], h_rows[:, t, 0:LOW])
        nc.sync.dma_start(h_high[0][:], h_rows[:, 0:2, LOW:E])
        nc.sync.dma_start(h_high[1][:], h_rows[:, 2:3, LOW:E])
        nc.sync.dma_start(w_raw[:], wm.rearrange("(p j) d -> p j d", j=PACK))
        nc.sync.dma_start(h_high[2][:], h_rows[:, 3:4, LOW:E])
        nc.sync.dma_start(src[:], offs2)

        identity = keep.tile([P, P], F32, name="identity")
        make_identity(nc, identity[:])
        ew_low = psum.tile([P, SPREAD, P], F32, name="ew_low", tag="bank7")
        for c in range(SPREAD):
            nc.tensor.transpose(ew_low[:, c, :], ew_column[:, c : c + 1].to_broadcast([P, P]), identity[:])

        minus_half = keep.tile([P, 1], F32, name="minus_half")
        nc.gpsimd.memset(minus_half[:], -0.5)

        looked = [keep.tile([P, PACK, n], F32, name="looked%d" % s) for s, n in enumerate((LOW, HIGH))]
        for t in range(PACK):
            nc.scalar.activation(looked[0][:, t, :], dy[t][:].indirect(dst[:, 0 : LOW // 16]), ACT.Copy, scale=-1.0)
            for s, (e0, n) in enumerate(PIECES):
                high = dst[:, e0 // 16 : (e0 + n) // 16]
                nc.vector.tensor_tensor(
                    looked[1][:, t, e0 - LOW : e0 - LOW + n], dy[t][:].indirect(high), ew_high[s][:], ALU.mult
                )

        w_grouped = keep.tile([P, PACK * D], BF16, name="w_grouped", tag="grouped1", align_bytes=64)
        w_codes = keep.tile([P, D], U32, name="w_codes", align_bytes=64)
        w_scales = keep.tile([P, D], U8, name="w_scales", align_bytes=64)

        factor = [keep.tile([P, PACK, n], F32, name="factor%d" % s) for s, n in enumerate((LOW, HIGH))]
        for t in range(PACK):
            sq = keep.tile([P, LOW], F32, name="sq_low%d" % t)
            nc.scalar.activation(sq[:], h_low[t][:], ACT.Square, bias=minus_half[:])
            nc.vector.scalar_tensor_tensor(
                factor[0][:, t, :].rearrange("p (k c) -> p k c", c=SPREAD),
                sq[:].rearrange("p (k c) -> p k c", c=SPREAD),
                0.25,
                ew_low[:].rearrange("p c k -> p k c"),
                ALU.subtract,
                ALU.mult,
            )
        for q, (a, b) in enumerate(HIGH_PLANES):
            sq = keep.tile([P, b - a, HIGH], F32, name="sq_high%d" % q, tag="squares%d" % q)
            nc.scalar.activation(sq[:], h_high[q][:], ACT.Square, bias=minus_half[:])
            nc.scalar.activation(factor[1][:, a:b, :], sq[:], ACT.Copy, bias=0.25, scale=-1.0)

        dm = keep.tile([P, PACK, E], F32, name="dm", tag="squares2")
        dz_grouped = []
        late_copies = []
        banks = []

        def form_dz(c):
            e0, n = EDGE_CHUNKS[c]
            s, a = (0, e0) if e0 < LOW else (1, e0 - LOW)
            dz_grouped.append(keep.tile([P, PACK * n], BF16, name="dzg%d" % c, tag="grouped%d" % c, align_bytes=64))
            nc.vector.tensor_tensor(
                dz_grouped[c][:].rearrange("p (g i t) -> p g t i", i=2, t=PACK),
                looked[s][:, :, a : a + n].rearrange("p t (g i) -> p g t i", i=2),
                factor[s][:, :, a : a + n].rearrange("p t (g i) -> p g t i", i=2),
                ALU.mult,
            )

        def multiply(c):
            e0, n = EDGE_CHUNKS[c]
            codes = keep.tile([P, n], U32, name="dzc%d" % c, align_bytes=64)
            scales = keep.tile([P, n], U8, name="dzs%d" % c, align_bytes=64)
            nc.vector.quantize_mx(out=codes[:].bitcast(E5M2), scales=scales[:], in_=dz_grouped[c][:])
            per_bank = 2 if n > P or c == len(EDGE_CHUNKS) - 1 else PACK
            for t0 in range(0, PACK, per_bank):
                bank = psum.tile([P, per_bank, n], F32, name="bank%d%d" % (c, t0), tag="bank%d" % (len(banks) % 8))
                banks.append(bank)
                for u in range(per_bank):
                    cols = slice((t0 + u) * P, (t0 + u + 1) * P)
                    nc.tensor.matmul_mx(
                        out=bank[:, u, :],
                        lhsT=w_codes[:, cols].bitcast(E4M3),
                        lhsT_scale=w_scales[:, cols],
                        rhs=codes[:].bitcast(E5M2),
                        rhs_scale=scales[:],
                        start=True,
                        stop=True,
                    )
                target = dm[:, t0 : t0 + per_bank, e0 : e0 + n]
                if c >= 4 and t0 == 0:
                    late_copies.append((target, bank[:]))
                else:
                    nc.scalar.copy(target, bank[:])

        form_dz(0)
        w_to = w_grouped[:].rearrange("p (t m j) -> p m j t", t=PACK, j=PACK)
        w_from = w_raw[:].rearrange("p j (m t) -> p m j t", t=PACK)
        nc.vector.tensor_copy(w_to, w_from)
        nc.vector.quantize_mx(out=w_codes[:].bitcast(E4M3), scales=w_scales[:], in_=w_grouped[:])

        for c in range(1, len(EDGE_CHUNKS)):
            form_dz(c)
            multiply(c - 1)
        multiply(len(EDGE_CHUNKS) - 1)
        for target, source in late_copies:
            nc.vector.tensor_copy(target, source)

        out_rows = out_0.rearrange("(p t) x -> p t x", t=PACK)
        words_out = out_1[0].rearrange("p x l -> p (x l)").bitcast(I32)
        y_codes = keep.tile([P, V], U32, name="y_codes", align_bytes=64)
        y_scales = keep.tile([P, V], U8, name="y_scales", align_bytes=64)
        y_grouped = keep.tile([P, PACK * V], BF16, name="y_grouped", align_bytes=64)
        for k, (x0, n) in enumerate(NODE_CHUNKS):
            picked = keep.tile([P, PACK, 2 * n], F32, name="picked%d" % k)
            y = keep.tile([P, PACK, n], F32, name="y%d" % k)
            entries = src[:, 2 * x0 // 16 : 2 * (x0 + n) // 16]
            for t in (0, 2, 1, 3):
                if (k == 0 and t < 2) or (k == 2 and t < 2):
                    nc.vector.tensor_copy(picked[:, t, :], dm[:, t, :].indirect(entries))
                else:
                    nc.scalar.activation(picked[:, t, :], dm[:, t, :].indirect(entries), ACT.Copy)
            pairs = picked[:].rearrange("p t (x j) -> p t x j", j=2)
            for q in range(2):
                nc.vector.tensor_tensor(
                    y[:, 2 * q : 2 * q + 2, :], pairs[:, 2 * q : 2 * q + 2, :, 0], pairs[:, 2 * q : 2 * q + 2, :, 1], ALU.add
                )
            nc.sync.dma_start(out_rows[:, :, x0 : x0 + n], y[:])
            nc.vector.tensor_copy(
                y_grouped[:, PACK * x0 : PACK * (x0 + n)].rearrange("p (g i t) -> p g t i", i=2, t=PACK),
                y[:].rearrange("p t (g i) -> p g t i", i=2),
            )
            for a, b in PLANE_CHUNKS:
                if x0 < b <= x0 + n:
                    nc.vector.quantize_mx(
                        out=y_codes[:, a:b].bitcast(E4M3), scales=y_scales[:, a:b], in_=y_grouped[:, PACK * a : PACK * b]
                    )
                    (nc.scalar if b == V else nc.sync).dma_start(words_out[:, a:b], y_codes[:, a:b].bitcast(I32))
        scales_out = out_2[0].bitcast(I32)
        for quad in range(4):
            queue = nc.sync if quad % 2 == 0 else nc.scalar
            queue.dma_start(scales_out[4 * quad : 4 * quad + 4, :], y_scales[32 * quad : 32 * quad + 4, :].bitcast(I32))
